import numpy as np
CORES = [7,14,21,28,35,42,49,56,71,78,85,92,99,106,113,120]
N = 16
def setup_inputs(rng):
    return {"x": rng.standard_normal((N, 128, 128), dtype=np.float32)}
def reference(x):
    s = x.min(axis=0)
    return {"y": np.broadcast_to(s, (N,) + s.shape)}

@@ -1,0 +1,80 @@
+from concourse.bass import DstId, RemoteDMATransfer
+
+CH = [128, 4]
+
+SCRATCH = {
+    "xs": ("dram", [32] + CH, "float32"),
+    "xin": ("dram", [16] + CH, "float32"),
+    "xm": ("dram", [8] + CH, "float32"),
+    "part": ("dram", [8] + CH, "float32"),
+    "res": ("dram", [8] + CH, "float32"),
+    "yb": ("dram", [32] + CH, "float32"),
+}
+SEMAPHORES = ["ld", "st", "sent", "xin_arr", "xm_arr", "part_arr", "res_arr", "y_arr"]
+
+MIN = 3
+
+
+def roles(rank_core):
+    base, k = rank_core - rank_core % 8, rank_core % 8
+    ports = [base + (3 if k == 2 else 2), base + (7 if k == 6 else 6)]
+    folds = [base + (1 if k == 0 else 0), base + (5 if k == 4 else 4)]
+    return ports, folds
+
+
+def rank_program(g, core, T, topo):
+    chip = topo.chip(core)
+    p, q = chip & 1, chip >> 1
+    R = {topo.chip(c): c for c in T.cores}
+    P = {c: roles(R[c])[0] for c in R}
+    F = {c: roles(R[c])[1] for c in R}
+    mate = chip ^ 1
+    plane = [2 * j + p for j in range(8)]
+
+    def did(c):
+        rid, pid, _se = topo.addr(c)
+        return DstId(rid=rid, pnc=pid)
+
+    if core == R[chip]:
+        g.dma_start(T.xs[:], T.x[:]).then_inc(T.sem.ld, 16)
+        g.wait_ge(T.sem.ld, 16)
+        for s in range(2):
+            g.remote_dma_fused(
+                [RemoteDMATransfer(dst_ids=[did(P[chip][s])], dma_engine_mask=1 << i, remote_sem=T.sem.xin_arr,
+                                   src=T.xs[s * 16 + i], dst=T.xin[i]) for i in range(16)],
+                local_sem=T.sem.sent)
+        g.wait_ge(T.sem.y_arr, 32)
+        g.dma_start(T.y[:], T.yb[:]).then_inc(T.sem.st, 16)
+        g.wait_ge(T.sem.st, 16)
+        g.wait_ge(T.sem.sent, 32)
+        return
+
+    for s in range(2):
+        if core == P[chip][s]:
+            g.wait_ge(T.sem.xin_arr, 16)
+            g.remote_dma_fused(
+                [RemoteDMATransfer(dst_ids=[did(P[mate][s])], dma_engine_mask=1 << j, remote_sem=T.sem.xm_arr,
+                                   src=T.xin[(1 - p) * 8 + j], dst=T.xm[j]) for j in range(8)],
+                local_sem=T.sem.sent)
+            g.wait_ge(T.sem.xm_arr, 8)
+            g.remote_dma_fused(
+                [RemoteDMATransfer(dst_ids=[did(F[plane[j]][s])], dma_engine_mask=1 << j, remote_sem=T.sem.part_arr,
+                                   srcs=[T.xin[p * 8 + j], T.xm[j]], dsts=[T.part[q]], alu_op=MIN) for j in range(8)],
+                local_sem=T.sem.sent)
+            g.wait_ge(T.sem.res_arr, 64)
+            g.remote_dma_fused(
+                [RemoteDMATransfer(dst_ids=[did(R[chip]), did(R[mate])], dma_engine_mask=1 << j,
+                                   remote_sem=T.sem.y_arr, srcs=[T.res[j]],
+                                   dsts=[T.yb[s * 16 + p * 8 + j]] * 2) for j in range(8)],
+                local_sem=T.sem.sent)
+            g.wait_ge(T.sem.sent, 24)
+            return
+        if core == F[chip][s]:
+            g.wait_ge(T.sem.part_arr, 8)
+            g.remote_dma_fused(
+                [RemoteDMATransfer(dst_ids=[did(P[c][s]) for c in plane], dma_engine_mask=0xFF,
+                                   remote_sem=T.sem.res_arr, srcs=[T.part[j] for j in range(8)],
+                                   dsts=[T.res[q]] * 8, alu_op=MIN)],
+                local_sem=T.sem.sent)
+            g.wait_ge(T.sem.sent, 8)
+            return

@@ -4,13 +4,14 @@ CH = [128, 4]
 
 SCRATCH = {
     "xs": ("dram", [32] + CH, "float32"),
-    "xin": ("dram", [16] + CH, "float32"),
+    "xo": ("dram", [8] + CH, "float32"),
+    "xi": ("dram", [8] + CH, "float32"),
     "xm": ("dram", [8] + CH, "float32"),
     "part": ("dram", [8] + CH, "float32"),
     "res": ("dram", [8] + CH, "float32"),
     "yb": ("dram", [32] + CH, "float32"),
 }
-SEMAPHORES = ["ld", "st", "sent", "xin_arr", "xm_arr", "part_arr", "res_arr", "y_arr"]
+SEMAPHORES = ["ld_o", "ld_i", "st", "sent", "xo_arr", "xi_arr", "xm_arr", "part_arr", "res_arr", "y_arr"]
 
 MIN = 3
 
@@ -30,51 +31,55 @@ def rank_program(g, core, T, topo):
     F = {c: roles(R[c])[1] for c in R}
     mate = chip ^ 1
     plane = [2 * j + p for j in range(8)]
+    sem = T.sem
 
     def did(c):
         rid, pid, _se = topo.addr(c)
         return DstId(rid=rid, pnc=pid)
 
     if core == R[chip]:
-        g.dma_start(T.xs[:], T.x[:]).then_inc(T.sem.ld, 16)
-        g.wait_ge(T.sem.ld, 16)
-        for s in range(2):
+        o = 1 - p
+        g.sync.dma_start(T.xs[16 * o:16 * o + 16], T.x[64 * o:64 * o + 64, :]).then_inc(sem.ld_o, 16)
+        g.scalar.dma_start(T.xs[16 * p:16 * p + 16], T.x[64 * p:64 * p + 64, :]).then_inc(sem.ld_i, 16)
+        for h, ld, buf, arr in ((o, sem.ld_o, T.xo, sem.xo_arr), (p, sem.ld_i, T.xi, sem.xi_arr)):
+            g.wait_ge(ld, 16)
             g.remote_dma_fused(
-                [RemoteDMATransfer(dst_ids=[did(P[chip][s])], dma_engine_mask=1 << i, remote_sem=T.sem.xin_arr,
-                                   src=T.xs[s * 16 + i], dst=T.xin[i]) for i in range(16)],
-                local_sem=T.sem.sent)
-        g.wait_ge(T.sem.y_arr, 32)
-        g.dma_start(T.y[:], T.yb[:]).then_inc(T.sem.st, 16)
-        g.wait_ge(T.sem.st, 16)
-        g.wait_ge(T.sem.sent, 32)
+                [RemoteDMATransfer(dst_ids=[did(P[chip][s])], dma_engine_mask=1 << (s * 8 + j), remote_sem=arr,
+                                   src=T.xs[h * 16 + s * 8 + j], dst=buf[j]) for s in range(2) for j in range(8)],
+                local_sem=sem.sent)
+        g.sync.wait_ge(sem.y_arr, 32)
+        g.sync.dma_start(T.y[:], T.yb[:]).then_inc(sem.st, 16)
+        g.wait_ge(sem.sent, 32)
+        g.wait_ge(sem.st, 16)
         return
 
     for s in range(2):
         if core == P[chip][s]:
-            g.wait_ge(T.sem.xin_arr, 16)
+            g.wait_ge(sem.xo_arr, 8)
             g.remote_dma_fused(
-                [RemoteDMATransfer(dst_ids=[did(P[mate][s])], dma_engine_mask=1 << j, remote_sem=T.sem.xm_arr,
-                                   src=T.xin[(1 - p) * 8 + j], dst=T.xm[j]) for j in range(8)],
-                local_sem=T.sem.sent)
-            g.wait_ge(T.sem.xm_arr, 8)
+                [RemoteDMATransfer(dst_ids=[did(P[mate][s])], dma_engine_mask=1 << j, remote_sem=sem.xm_arr,
+                                   src=T.xo[j], dst=T.xm[j]) for j in range(8)],
+                local_sem=sem.sent)
+            g.wait_ge(sem.xi_arr, 8)
+            g.wait_ge(sem.xm_arr, 8)
             g.remote_dma_fused(
-                [RemoteDMATransfer(dst_ids=[did(F[plane[j]][s])], dma_engine_mask=1 << j, remote_sem=T.sem.part_arr,
-                                   srcs=[T.xin[p * 8 + j], T.xm[j]], dsts=[T.part[q]], alu_op=MIN) for j in range(8)],
-                local_sem=T.sem.sent)
-            g.wait_ge(T.sem.res_arr, 64)
+                [RemoteDMATransfer(dst_ids=[did(F[plane[j]][s])], dma_engine_mask=1 << j, remote_sem=sem.part_arr,
+                                   srcs=[T.xi[j], T.xm[j]], dsts=[T.part[q]], alu_op=MIN) for j in range(8)],
+                local_sem=sem.sent)
+            g.wait_ge(sem.res_arr, 8)
             g.remote_dma_fused(
-                [RemoteDMATransfer(dst_ids=[did(R[chip]), did(R[mate])], dma_engine_mask=1 << j,
-                                   remote_sem=T.sem.y_arr, srcs=[T.res[j]],
-                                   dsts=[T.yb[s * 16 + p * 8 + j]] * 2) for j in range(8)],
-                local_sem=T.sem.sent)
-            g.wait_ge(T.sem.sent, 24)
+                [RemoteDMATransfer(dst_ids=[did(dst)], dma_engine_mask=1 << (e + j), remote_sem=sem.y_arr,
+                                   src=T.res[j], dst=T.yb[p * 16 + s * 8 + j])
+                 for dst, e in ((R[mate], 0), (R[chip], 8)) for j in range(8)],
+                local_sem=sem.sent)
+            g.wait_ge(sem.sent, 32)
             return
         if core == F[chip][s]:
-            g.wait_ge(T.sem.part_arr, 8)
+            g.wait_ge(sem.part_arr, 8)
             g.remote_dma_fused(
-                [RemoteDMATransfer(dst_ids=[did(P[c][s]) for c in plane], dma_engine_mask=0xFF,
-                                   remote_sem=T.sem.res_arr, srcs=[T.part[j] for j in range(8)],
-                                   dsts=[T.res[q]] * 8, alu_op=MIN)],
-                local_sem=T.sem.sent)
-            g.wait_ge(T.sem.sent, 8)
+                [RemoteDMATransfer(dst_ids=[did(P[plane[j]][s])], dma_engine_mask=1 << j, remote_sem=sem.res_arr,
+                                   srcs=[T.part[i] for i in range(8)], dsts=[T.res[q]], alu_op=MIN)
+                 for j in range(8)],
+                local_sem=sem.sent)
+            g.wait_ge(sem.sent, 8)
             return

from concourse.bass import DstId, RemoteDMATransfer

CH = [128, 4]

SCRATCH = {
    "xs": ("dram", [32] + CH, "float32"),
    "xo": ("dram", [8] + CH, "float32"),
    "xi": ("dram", [8] + CH, "float32"),
    "xm": ("dram", [8] + CH, "float32"),
    "part": ("dram", [8] + CH, "float32"),
    "res": ("dram", [8] + CH, "float32"),
    "yb": ("dram", [32] + CH, "float32"),
}
SEMAPHORES = ["ld_o", "ld_i", "st", "sent", "xo_arr", "xi_arr", "xm_arr", "part_arr", "res_arr", "y_arr"]

MIN = 3


def roles(rank_core):
    base, k = rank_core - rank_core % 8, rank_core % 8
    ports = [base + (3 if k == 2 else 2), base + (7 if k == 6 else 6)]
    folds = [base + (1 if k == 0 else 0), base + (5 if k == 4 else 4)]
    return ports, folds


def rank_program(g, core, T, topo):
    chip = topo.chip(core)
    p, q = chip & 1, chip >> 1
    R = {topo.chip(c): c for c in T.cores}
    P = {c: roles(R[c])[0] for c in R}
    F = {c: roles(R[c])[1] for c in R}
    mate = chip ^ 1
    plane = [2 * j + p for j in range(8)]
    sem = T.sem

    def did(c):
        rid, pid, _se = topo.addr(c)
        return DstId(rid=rid, pnc=pid)

    if core == R[chip]:
        o = 1 - p
        g.sync.dma_start(T.xs[16 * o:16 * o + 16], T.x[64 * o:64 * o + 64, :]).then_inc(sem.ld_o, 16)
        g.scalar.dma_start(T.xs[16 * p:16 * p + 16], T.x[64 * p:64 * p + 64, :]).then_inc(sem.ld_i, 16)
        for h, ld, buf, arr in ((o, sem.ld_o, T.xo, sem.xo_arr), (p, sem.ld_i, T.xi, sem.xi_arr)):
            g.wait_ge(ld, 16)
            g.remote_dma_fused(
                [RemoteDMATransfer(dst_ids=[did(P[chip][s])], dma_engine_mask=1 << (s * 8 + j), remote_sem=arr,
                                   src=T.xs[h * 16 + s * 8 + j], dst=buf[j]) for s in range(2) for j in range(8)],
                local_sem=sem.sent)
        g.sync.wait_ge(sem.y_arr, 32)
        g.sync.dma_start(T.y[:], T.yb[:]).then_inc(sem.st, 16)
        g.wait_ge(sem.sent, 32)
        g.wait_ge(sem.st, 16)
        return

    for s in range(2):
        if core == P[chip][s]:
            g.wait_ge(sem.xo_arr, 8)
            g.remote_dma_fused(
                [RemoteDMATransfer(dst_ids=[did(P[mate][s])], dma_engine_mask=1 << j, remote_sem=sem.xm_arr,
                                   src=T.xo[j], dst=T.xm[j]) for j in range(8)],
                local_sem=sem.sent)
            g.wait_ge(sem.xi_arr, 8)
            g.wait_ge(sem.xm_arr, 8)
            g.remote_dma_fused(
                [RemoteDMATransfer(dst_ids=[did(F[plane[j]][s])], dma_engine_mask=1 << j, remote_sem=sem.part_arr,
                                   srcs=[T.xi[j], T.xm[j]], dsts=[T.part[q]], alu_op=MIN) for j in range(8)],
                local_sem=sem.sent)
            g.wait_ge(sem.res_arr, 8)
            g.remote_dma_fused(
                [RemoteDMATransfer(dst_ids=[did(dst)], dma_engine_mask=1 << (e + j), remote_sem=sem.y_arr,
                                   src=T.res[j], dst=T.yb[p * 16 + s * 8 + j])
                 for dst, e in ((R[mate], 0), (R[chip], 8)) for j in range(8)],
                local_sem=sem.sent)
            g.wait_ge(sem.sent, 32)
            return
        if core == F[chip][s]:
            g.wait_ge(sem.part_arr, 8)
            g.remote_dma_fused(
                [RemoteDMATransfer(dst_ids=[did(P[plane[j]][s])], dma_engine_mask=1 << j, remote_sem=sem.res_arr,
                                   srcs=[T.part[i] for i in range(8)], dsts=[T.res[q]], alu_op=MIN)
                 for j in range(8)],
                local_sem=sem.sent)
            g.wait_ge(sem.sent, 8)
            return
